import numpy as np
import ml_dtypes


def mxq(x, axis, fmt="e4m3"):
    dtype, down = {"e4m3": (ml_dtypes.float8_e4m3fn, 7), "e5m2": (ml_dtypes.float8_e5m2, 14)}[fmt]
    v = np.moveaxis(np.asarray(x, np.float32).astype(ml_dtypes.bfloat16).astype(np.float64), axis, -1)
    blocks = v.reshape(v.shape[:-1] + (-1, 32))
    amax = np.abs(blocks).max(-1, keepdims=True)
    byte = np.maximum(np.where(amax > 0, np.frexp(amax)[1] - 1 + 127, 0) - down, 1)
    scale = np.exp2(byte - 127.0)
    codes = (blocks / scale).astype(np.float32).astype(dtype).astype(np.float64)
    return np.moveaxis((codes * scale).reshape(v.shape), -1, axis)


WIDE = False


def mx_kscale(k):
    if not WIDE:
        return np.ones(k)
    levels = np.array([10, -10, 5, -5, 0])
    if k % 512:
        return np.exp2(np.random.permutation(np.resize(levels, k // 32))).repeat(32)
    a = np.empty((k // 512, 16))
    for p in range(k // 512):
        a[p, :8] = np.random.permutation(np.resize(levels, 8))
        for g in range(8):
            far = levels[np.abs(levels - a[p, g]) >= 10]
            a[p, g + 8] = far[np.random.randint(len(far))]
    return np.exp2(a.ravel()).repeat(32)


def f64(x):
    return np.asarray(x).astype(np.float64)


def striped(idx):
    return np.tile(idx.reshape(-1, 16).T, (8, 1)).astype(np.uint16)


def unstriped(offs):
    return offs[:16].T.reshape(-1).astype(np.int64)


def striped8(idx):
    return np.concatenate([x.reshape(-1, 16).T for x in idx]).astype(np.uint16)


def runs(offs, k):
    lists = np.stack([offs[16 * r : 16 * r + 16].T.reshape(-1) for r in range(8)]).astype(np.int64)
    return lists[np.arange(k) % 512 // 64]


def pack_weight(w):
    k, n = w.shape
    w = f64(np.asarray(w, np.float32).astype(ml_dtypes.bfloat16)).reshape(k // 32, 32, n)
    amax = np.abs(w).max(1)
    byte = np.clip(np.where(amax > 0, np.frexp(amax)[1] - 1 + 127 - 7, 1), 1, 254)
    scaled = (w * np.exp2(127.0 - byte)[:, None, :]).reshape(k, n).astype(np.float32)
    words = np.ascontiguousarray(scaled.reshape(k // 512, 128, 4, n).transpose(0, 1, 3, 2)).astype(ml_dtypes.float8_e4m3fn).view(np.uint8)
    return words, np.ascontiguousarray(byte.astype(np.uint8).reshape(k // 512, 16, n))


def unpack_weight(words, scales):
    g, p, n, _ = words.shape
    vals = np.ascontiguousarray(words).view(ml_dtypes.float8_e4m3fn).astype(np.float64) * np.repeat(np.exp2(scales.astype(np.float64) - 127.0), 8, axis=1)[..., None]
    return vals.transpose(0, 1, 3, 2).reshape(g * 512, n)


def sigmoid(v):
    return 1.0 / (1.0 + np.exp(-np.maximum(v, -700.0)))

def planes(y):
    n, m = y.shape
    v = y.astype(np.float32).astype(ml_dtypes.bfloat16).astype(np.float64).reshape(n // 32, 32, m)
    top = np.abs(v).max(1)
    byte = np.clip(np.where(top > 0, np.frexp(top)[1] - 1 + 127 - 7, 1), 1, 254)
    codes = (v * np.exp2(127.0 - byte)[:, None, :]).reshape(n, m).astype(np.float32).astype(ml_dtypes.float8_e4m3fn).view(np.uint8)
    words = codes.reshape(n // 512, 128, 4, m).transpose(0, 1, 3, 2)
    return np.ascontiguousarray(words), np.ascontiguousarray(byte.astype(np.uint8).reshape(n // 512, 16, m))


K, T, S, N, G, H, W, U = 512, 2048, 512, 512, 2048, 512, 1024, 384


def setup_inputs():
    n = np.random.standard_normal
    s = mx_kscale(K)[:, None]
    u = mx_kscale(S)
    packed_xT = pack_weight(n((K, T)) * s)
    packed_dT = pack_weight(n((K, G)) / s)
    packed_w1 = pack_weight(n((H, N)) / np.sqrt(H) / u[:, None])
    return {
        "x_words": packed_xT[0],
        "x_scales": packed_xT[1],
        "d_words": packed_dT[0],
        "d_scales": packed_dT[1],
        "gn": (np.random.uniform(0.5, 1.5, (H, 1)) * u[:, None]).astype(np.float32),
        "w1_words": packed_w1[0],
        "w1_scales": packed_w1[1],
        "offs": striped8(np.random.randint(0, T, (8, S))),
        "k1": striped8(np.random.randint(0, G, (8, H))),
        "n1": striped(np.random.randint(0, S, W)),
        "n2": striped(np.random.permutation(S)),
        "n3": striped(np.random.permutation(S)[:U]),
        "n4": striped(np.random.permutation(S)[:U]),
    }


def reference(x_words, x_scales, d_words, d_scales, gn, w1_words, w1_scales, offs, k1, n1, n2, n3, n4):
    d_k1 = unpack_weight(d_words, d_scales)[np.arange(K)[:, None], runs(k1, K)]
    xq = unpack_weight(x_words, x_scales)[np.arange(K)[:, None], runs(offs, K)]
    h = 0.0625 * (d_k1.T @ xq)
    mb = h[:, unstriped(n1)]
    mx = mb.reshape(H, S, 2).max(axis=2)
    st = h - mx
    z = f64(gn) * (np.maximum(st, st[:, unstriped(n2)]))
    h2 = unpack_weight(w1_words, w1_scales).T @ mxq(z, 0, "e4m3")
    old = h2[:, unstriped(n3)]
    pa = h2[:, unstriped(n4)]
    ra = old * sigmoid(pa)
    out = h2.copy()
    out[:, unstriped(n3)] = ra
    return (out,) + planes(out)

@@ -1,0 +1,228 @@
+from contextlib import ExitStack
+
+import concourse.mybir as mybir
+
+F32 = mybir.dt.float32
+BF16 = mybir.dt.bfloat16
+U32 = mybir.dt.uint32
+I32 = mybir.dt.int32
+U16 = mybir.dt.uint16
+U8 = mybir.dt.uint8
+FP8X4 = mybir.dt.float8_e4m3fn_x4
+ALU = mybir.AluOpType
+ACT = mybir.ActivationFunctionType
+
+P = 128
+PACK = 4
+S = 512
+HALF = 256
+TABLE = 2048
+U = 384
+SPARE = 16
+FLOPS = 2 * 2 * 512 * 512 * 512
+CFG = {"E":"SSSV","ga":"VVVS","gb":"SSSS","n":"VSSSSSSS","sc":"SSSSSSSS","il":"VV","F":"SVVVVVVV","P":"YVYS","C":"VS","K":"VVVV"}
+
+
+def tile_picked_hpqghopmkgate_none_po_kernel(
+    tc, x_words, x_scales, d_words, d_scales, gn, w1_words, w1_scales, offs, k1, n1, n2, n3, n4, out_0, out_1, out_2
+):
+    nc = tc.nc
+    with ExitStack() as ctx:
+        keep = ctx.enter_context(tc.tile_pool(name="keep", bufs=1))
+        psum = ctx.enter_context(tc.psum_pool(name="psum", bufs=1))
+
+        def sb(name, shape, dtype):
+            return keep.tile(shape, dtype, name=name, align_bytes=64)
+
+        def words_of(dram):
+            return dram[0].rearrange("p n t -> p (n t)").bitcast(I32)
+
+        def half(h):
+            return slice(HALF * h, HALF * (h + 1))
+
+        k1_t = sb("k1_t", [P, 32], U16)
+        offs_t = sb("offs_t", [P, 32], U16)
+        n1_t = sb("n1_t", [P, 64], U16)
+        n2_t = sb("n2_t", [P, 32], U16)
+        n3_t = sb("n3_t", [P, 24], U16)
+        n4_t = sb("n4_t", [P, 24], U16)
+        d_tab = sb("d_tab", [P, TABLE], U32)
+        x_tab = sb("x_tab", [P, TABLE], U32)
+        d_stab = sb("d_stab", [P, TABLE], U8)
+        x_stab = sb("x_stab", [P, TABLE], U8)
+        w_raw = sb("w_raw", [P, S], U32)
+        w_sraw = sb("w_sraw", [P, S], U8)
+        gain = sb("gain", [P, PACK], F32)
+
+        nc.vector.memset(d_stab[:].bitcast(I32), 0)
+        nc.vector.memset(x_stab[:].bitcast(I32), 0)
+        nc.gpsimd.memset(w_sraw[:].bitcast(I32), 0)
+
+        nc.scalar.dma_start(gain[:], gn.rearrange("(p t) o -> p (t o)", t=PACK))
+        nc.scalar.dma_start(d_tab[:].bitcast(I32), words_of(d_words))
+        nc.scalar.dma_start(x_tab[:].bitcast(I32), words_of(x_words))
+        nc.sync.dma_start(k1_t[:], k1)
+        nc.sync.dma_start(offs_t[:], offs)
+        nc.sync.dma_start(d_stab[0:P:8, :].bitcast(I32), d_scales[0].bitcast(I32))
+        nc.sync.dma_start(x_stab[0:P:8, :].bitcast(I32), x_scales[0].bitcast(I32))
+
+        d_sg = sb("d_sg", [P, S], U8)
+        x_sg = sb("x_sg", [P, S], U8)
+        planes = sb("planes", [P, 2 * S], U8)
+        nc.vector.tensor_copy(d_sg[:], d_stab[:].indirect(k1_t[:]))
+        nc.vector.tensor_copy(x_sg[:], x_stab[:].indirect(offs_t[:]))
+        nc.vector.tensor_copy(
+            planes[:, 0:S].rearrange("p (t m) -> p t m", t=PACK), d_sg[:].rearrange("p (m t) -> p t m", t=PACK)
+        )
+        nc.vector.tensor_copy(planes[:, S : 2 * S].bitcast(I32), x_sg[:].bitcast(I32))
+        for a in range(1, 4):
+            nc.sync.dma_start(planes[a:P:32, :].bitcast(I32), planes[8 * a : P : 32, :].bitcast(I32))
+
+        nc.sync.dma_start(n1_t[:], n1)
+        nc.sync.dma_start(n2_t[:], n2)
+        nc.sync.dma_start(n3_t[:], n3)
+        nc.sync.dma_start(n4_t[:], n4)
+        for q in range(4):
+            nc.gpsimd.dma_start(w_sraw[32 * q : 32 * q + 4, :].bitcast(I32), w1_scales[0, 4 * q : 4 * q + 4, :].bitcast(I32))
+        nc.scalar.dma_start(w_raw[:].bitcast(I32), words_of(w1_words))
+
+        def deal_words(dst, src):
+            nc.vector.tensor_copy(
+                dst[:].rearrange("p (t c i) -> p c t i", t=PACK, i=4), src[:].rearrange("p (c i t) -> p c t i", t=PACK, i=4)
+            )
+
+        d_g = sb("d_g", [P, S], U32)
+        d_dealt = sb("d_dealt", [P, S], U32)
+        x_g = [sb("x_g%d" % h, [P, HALF], U32) for h in range(2)]
+        nc.vector.tensor_copy(d_g[:], d_tab[:].indirect(k1_t[:]))
+        deal_words(d_dealt, d_g)
+        for h in range(2):
+            nc.vector.tensor_copy(x_g[h][:], x_tab[:].indirect(offs_t[:, 16 * h : 16 * (h + 1)]))
+
+        hh = [sb("h%d" % t, [P, S + SPARE], F32) for t in range(PACK)]
+        st = [sb("st%d" % t, [P, S], F32) for t in range(PACK)]
+        for t in range(PACK):
+            nc.vector.memset(hh[t][:, S:], 0.0)
+
+        acc1 = {}
+        for t in range(PACK):
+            for h in range(2):
+                acc1[t, h] = psum.tile([P, HALF], F32, name="acc1_%d_%d" % (t, h), tag="bank%d_%d" % (t, h))
+                nc.tensor.matmul_mx(
+                    out=acc1[t, h][:],
+                    lhsT=d_dealt[:, P * t : P * (t + 1)].bitcast(FP8X4),
+                    lhsT_scale=planes[:, P * t : P * (t + 1)],
+                    rhs=x_g[h][:].bitcast(FP8X4),
+                    rhs_scale=planes[:, S + HALF * h : S + HALF * (h + 1)],
+                    start=True,
+                    stop=True,
+                )
+
+        w_dealt = sb("w_dealt", [P, S], U32)
+        w_plane = sb("w_plane", [P, S], U8)
+        deal_words(w_dealt, w_raw)
+        nc.gpsimd.tensor_copy(
+            w_plane[:].rearrange("p (t m) -> p t m", t=PACK), w_sraw[:].rearrange("p (m t) -> p t m", t=PACK)
+        )
+
+        mb = [sb("mb%d" % t, [P, 2 * S], F32) for t in range(PACK)]
+        mx = [sb("mx%d" % t, [P, S], F32) for t in range(PACK)]
+
+        def gather(eng, out, window, offsets):
+            if eng == "S":
+                nc.scalar.activation(out, window.indirect(offsets), ACT.Copy)
+            else:
+                nc.vector.tensor_copy(out, window.indirect(offsets))
+
+        def scaled(eng, out, in_, scale):
+            if eng == "S":
+                nc.scalar.activation(out, in_, ACT.Copy, scale=scale)
+            else:
+                nc.vector.tensor_scalar(out, in_, scale, None, ALU.mult)
+
+        def copy(eng, out, in_):
+            if eng == "S":
+                nc.scalar.copy(out, in_)
+            else:
+                nc.vector.tensor_copy(out, in_)
+
+        def interleave(eng, out, rows):
+            copy(eng, out.rearrange("p (c i) t -> p c t i", i=4), rows.rearrange("p t (c i) -> p c t i", i=4))
+
+        def front(t):
+            for h in range(2):
+                scaled(CFG["E"][t], hh[t][:, half(h)], acc1[t, h][:], 0.0625)
+            gather(CFG["ga"][t], mb[t][:, 0:S], hh[t][:], n1_t[:, 0:32])
+            gather(CFG["gb"][t], mb[t][:, S : 2 * S], hh[t][:], n1_t[:, 32:64])
+
+        def mid(t):
+            pairs = mb[t][:].rearrange("p (j two) -> p j two", two=2)
+            nc.vector.tensor_tensor(mx[t][:], pairs[:, :, 0], pairs[:, :, 1], ALU.max)
+            nc.vector.tensor_tensor(st[t][:], hh[t][:, 0:S], mx[t][:], ALU.subtract)
+
+        for s in range(PACK + 1):
+            if s < PACK:
+                front(s)
+            if s > 0:
+                mid(s - 1)
+
+        y = [sb("y%d" % t, [P, S], F32) for t in range(PACK)]
+        for h in range(2):
+            z_rows = sb("z_rows%d" % h, [P, PACK, HALF], BF16)
+            z = sb("z%d" % h, [P, HALF, PACK], BF16)
+            z_codes = sb("z_codes%d" % h, [P, HALF], U32)
+            z_plane = sb("z_plane%d" % h, [P, HALF], U8)
+            for t in range(PACK):
+                other = sb("other%d_%d" % (t, h), [P, HALF], F32)
+                big = sb("big%d_%d" % (t, h), [P, HALF], F32)
+                gather(CFG["n"][4 * h + t], other[:], st[t][:], n2_t[:, 16 * h : 16 * (h + 1)])
+                nc.vector.tensor_tensor(big[:], st[t][:, half(h)], other[:], ALU.max)
+                scaled(CFG["sc"][4 * h + t], z_rows[:, t, :], big[:], gain[:, t : t + 1])
+            interleave(CFG["il"][h], z[:], z_rows[:])
+            nc.vector.quantize_mx(out=z_codes[:].bitcast(FP8X4), scales=z_plane[:], in_=z[:].rearrange("p j t -> p (j t)"))
+            acc2 = []
+            for t in range(PACK):
+                acc = psum.tile([P, HALF], F32, name="acc2_%d_%d" % (t, h), tag="bank%d_%d" % (t, h))
+                acc2.append(acc)
+                nc.tensor.matmul_mx(
+                    out=acc[:],
+                    lhsT=w_dealt[:, P * t : P * (t + 1)].bitcast(FP8X4),
+                    lhsT_scale=w_plane[:, P * t : P * (t + 1)],
+                    rhs=z_codes[:].bitcast(FP8X4),
+                    rhs_scale=z_plane[:],
+                    start=True,
+                    stop=True,
+                )
+            for t in range(PACK):
+                copy(CFG["F"][4 * h + t], y[t][:, half(h)], acc2[t][:])
+
+        old = [sb("old%d" % t, [P, U], F32) for t in range(PACK)]
+        gate = [sb("gate%d" % t, [P, U], F32) for t in range(PACK)]
+        y_rows = sb("y_rows", [P, PACK, S], BF16)
+        out_rows = out_0.rearrange("(p t) j -> p t j", t=PACK)
+        for t in range(PACK):
+            for u in range(2):
+                nc.scalar.activation(gate[t][:, 192 * u : 192 * (u + 1)], y[t][:].indirect(n4_t[:, 12 * u : 12 * (u + 1)]), ACT.Sigmoid)
+            if CFG["P"][t] == "Y":
+                nc.vector.tensor_tensor(old[t][:], y[t][:].indirect(n3_t[:]), gate[t][:], ALU.mult)
+            else:
+                gather(CFG["P"][t], old[t][:], y[t][:], n3_t[:])
+        for t in range(PACK):
+            if CFG["P"][t] == "Y":
+                nc.scalar.activation(y[t][:].indirect(n3_t[:]), old[t][:], ACT.Copy)
+            else:
+                nc.vector.tensor_tensor(y[t][:].indirect(n3_t[:]), old[t][:], gate[t][:], ALU.mult)
+            nc.sync.dma_start(out_rows[:, t, :], y[t][:])
+        for t in range(PACK):
+            copy(CFG["K"][t], y_rows[:, t, :], y[t][:])
+
+        y_plane = sb("y_plane", [P, S], U8)
+        for h in range(2):
+            y_bf = sb("y_bf%d" % h, [P, HALF, PACK], BF16)
+            y_codes = sb("y_codes%d" % h, [P, HALF], U32)
+            interleave(CFG["C"][h], y_bf[:], y_rows[:, :, half(h)])
+            nc.vector.quantize_mx(out=y_codes[:].bitcast(FP8X4), scales=y_plane[:, half(h)], in_=y_bf[:].rearrange("p j t -> p (j t)"))
+            nc.sync.dma_start(words_of(out_1)[:, half(h)], y_codes[:].bitcast(I32))
+        for q in range(4):
+            eng = nc.sync if q % 2 else nc.scalar
+            eng.dma_start(out_2[0, 4 * q : 4 * q + 4, :].bitcast(I32), y_plane[32 * q : 32 * q + 4, :].bitcast(I32))

@@ -20,7 +20,7 @@ TABLE = 2048
 U = 384
 SPARE = 16
 FLOPS = 2 * 2 * 512 * 512 * 512
-CFG = {"E":"SSSV","ga":"VVVS","gb":"SSSS","n":"VSSSSSSS","sc":"SSSSSSSS","il":"VV","F":"SVVVVVVV","P":"YVYS","C":"VS","K":"VVVV"}
+CFG = {"E":"SSSS","ga":"VVVV","gb":"SSSS","n":"SSSSSSSS","sc":"SSSSSSSS","zi":"00","il":"VV","F":"SSSSVVVV","P":"YYVS","C":"VV","K":"VVSV","ne":"4","warm":1,"cut":256}
 
 
 def tile_picked_hpqghopmkgate_none_po_kernel(
@@ -54,18 +54,21 @@ def tile_picked_hpqghopmkgate_none_po_kernel(
         w_sraw = sb("w_sraw", [P, S], U8)
         gain = sb("gain", [P, PACK], F32)
 
-        nc.vector.memset(d_stab[:].bitcast(I32), 0)
+        nc.gpsimd.memset(d_stab[:].bitcast(I32), 0)
         nc.vector.memset(x_stab[:].bitcast(I32), 0)
         nc.gpsimd.memset(w_sraw[:].bitcast(I32), 0)
 
         nc.scalar.dma_start(gain[:], gn.rearrange("(p t) o -> p (t o)", t=PACK))
-        nc.scalar.dma_start(d_tab[:].bitcast(I32), words_of(d_words))
-        nc.scalar.dma_start(x_tab[:].bitcast(I32), words_of(x_words))
         nc.sync.dma_start(k1_t[:], k1)
         nc.sync.dma_start(offs_t[:], offs)
         nc.sync.dma_start(d_stab[0:P:8, :].bitcast(I32), d_scales[0].bitcast(I32))
         nc.sync.dma_start(x_stab[0:P:8, :].bitcast(I32), x_scales[0].bitcast(I32))
+        nc.sync.dma_start(d_tab[:].bitcast(I32), words_of(d_words))
+        nc.sync.dma_start(n1_t[:], n1)
+        nc.sync.dma_start(x_tab[:].bitcast(I32), words_of(x_words))
 
+        warm = sb("warm", [P, 1], F32)
+        nc.scalar.activation(warm[:], gain[:, 0:1], ACT.Sigmoid)
         d_sg = sb("d_sg", [P, S], U8)
         x_sg = sb("x_sg", [P, S], U8)
         planes = sb("planes", [P, 2 * S], U8)
@@ -78,13 +81,12 @@ def tile_picked_hpqghopmkgate_none_po_kernel(
         for a in range(1, 4):
             nc.sync.dma_start(planes[a:P:32, :].bitcast(I32), planes[8 * a : P : 32, :].bitcast(I32))
 
-        nc.sync.dma_start(n1_t[:], n1)
+        nc.sync.dma_start(w_raw[:].bitcast(I32), words_of(w1_words))
         nc.sync.dma_start(n2_t[:], n2)
         nc.sync.dma_start(n3_t[:], n3)
         nc.sync.dma_start(n4_t[:], n4)
         for q in range(4):
-            nc.gpsimd.dma_start(w_sraw[32 * q : 32 * q + 4, :].bitcast(I32), w1_scales[0, 4 * q : 4 * q + 4, :].bitcast(I32))
-        nc.scalar.dma_start(w_raw[:].bitcast(I32), words_of(w1_words))
+            nc.sync.dma_start(w_sraw[32 * q : 32 * q + 4, :].bitcast(I32), w1_scales[0, 4 * q : 4 * q + 4, :].bitcast(I32))
 
         def deal_words(dst, src):
             nc.vector.tensor_copy(
@@ -121,7 +123,7 @@ def tile_picked_hpqghopmkgate_none_po_kernel(
         w_dealt = sb("w_dealt", [P, S], U32)
         w_plane = sb("w_plane", [P, S], U8)
         deal_words(w_dealt, w_raw)
-        nc.gpsimd.tensor_copy(
+        nc.vector.tensor_copy(
             w_plane[:].rearrange("p (t m) -> p t m", t=PACK), w_sraw[:].rearrange("p (m t) -> p t m", t=PACK)
         )
 
@@ -166,19 +168,30 @@ def tile_picked_hpqghopmkgate_none_po_kernel(
             if s > 0:
                 mid(s - 1)
 
-        y = [sb("y%d" % t, [P, S], F32) for t in range(PACK)]
+        y = [sb("y%d" % t, [P, 2 * U], F32) for t in range(PACK)]
+        for t in range(PACK):
+            nc.vector.memset(y[t][:, S:], 0.0)
         for h in range(2):
             z_rows = sb("z_rows%d" % h, [P, PACK, HALF], BF16)
             z = sb("z%d" % h, [P, HALF, PACK], BF16)
             z_codes = sb("z_codes%d" % h, [P, HALF], U32)
             z_plane = sb("z_plane%d" % h, [P, HALF], U8)
+            big = sb("big%d" % h, [P, PACK, HALF], F32)
             for t in range(PACK):
                 other = sb("other%d_%d" % (t, h), [P, HALF], F32)
-                big = sb("big%d_%d" % (t, h), [P, HALF], F32)
                 gather(CFG["n"][4 * h + t], other[:], st[t][:], n2_t[:, 16 * h : 16 * (h + 1)])
-                nc.vector.tensor_tensor(big[:], st[t][:, half(h)], other[:], ALU.max)
-                scaled(CFG["sc"][4 * h + t], z_rows[:, t, :], big[:], gain[:, t : t + 1])
-            interleave(CFG["il"][h], z[:], z_rows[:])
+                nc.vector.tensor_tensor(big[:, t, :], st[t][:, half(h)], other[:], ALU.max)
+                if CFG["zi"][h] == "0":
+                    scaled(CFG["sc"][4 * h + t], z_rows[:, t, :], big[:, t, :], gain[:, t : t + 1])
+            if CFG["zi"][h] == "0":
+                interleave(CFG["il"][h], z[:], z_rows[:])
+            else:
+                nc.vector.tensor_tensor(
+                    z[:].rearrange("p (c i) t -> p c t i", i=4),
+                    big[:].rearrange("p t (c i) -> p c t i", i=4),
+                    gain[:].unsqueeze(1).unsqueeze(3).to_broadcast([P, HALF // 4, PACK, 4]),
+                    ALU.mult,
+                )
             nc.vector.quantize_mx(out=z_codes[:].bitcast(FP8X4), scales=z_plane[:], in_=z[:].rearrange("p j t -> p (j t)"))
             acc2 = []
             for t in range(PACK):
@@ -201,8 +214,7 @@ def tile_picked_hpqghopmkgate_none_po_kernel(
         y_rows = sb("y_rows", [P, PACK, S], BF16)
         out_rows = out_0.rearrange("(p t) j -> p t j", t=PACK)
         for t in range(PACK):
-            for u in range(2):
-                nc.scalar.activation(gate[t][:, 192 * u : 192 * (u + 1)], y[t][:].indirect(n4_t[:, 12 * u : 12 * (u + 1)]), ACT.Sigmoid)
+            nc.scalar.activation(gate[t][:], y[t][:].indirect(n4_t[:]), ACT.Sigmoid)
             if CFG["P"][t] == "Y":
                 nc.vector.tensor_tensor(old[t][:], y[t][:].indirect(n3_t[:]), gate[t][:], ALU.mult)
             else:
@@ -212,17 +224,19 @@ def tile_picked_hpqghopmkgate_none_po_kernel(
                 nc.scalar.activation(y[t][:].indirect(n3_t[:]), old[t][:], ACT.Copy)
             else:
                 nc.vector.tensor_tensor(y[t][:].indirect(n3_t[:]), old[t][:], gate[t][:], ALU.mult)
-            nc.sync.dma_start(out_rows[:, t, :], y[t][:])
-        for t in range(PACK):
-            copy(CFG["K"][t], y_rows[:, t, :], y[t][:])
+            nc.sync.dma_start(out_rows[:, t, :], y[t][:, 0:S])
+        early = int(CFG["ne"])
+        for t in range(early):
+            copy(CFG["K"][t], y_rows[:, t, :], y[t][:, 0:S])
 
         y_plane = sb("y_plane", [P, S], U8)
-        for h in range(2):
-            y_bf = sb("y_bf%d" % h, [P, HALF, PACK], BF16)
-            y_codes = sb("y_codes%d" % h, [P, HALF], U32)
-            interleave(CFG["C"][h], y_bf[:], y_rows[:, :, half(h)])
-            nc.vector.quantize_mx(out=y_codes[:].bitcast(FP8X4), scales=y_plane[:, half(h)], in_=y_bf[:].rearrange("p j t -> p (j t)"))
-            nc.sync.dma_start(words_of(out_1)[:, half(h)], y_codes[:].bitcast(I32))
+        cut = CFG["cut"]
+        for h, (lo, hi) in enumerate([(0, cut), (cut, S)]):
+            y_bf = sb("y_bf%d" % h, [P, hi - lo, PACK], BF16)
+            y_codes = sb("y_codes%d" % h, [P, hi - lo], U32)
+            interleave(CFG["C"][h], y_bf[:], y_rows[:, :, lo:hi])
+            nc.vector.quantize_mx(out=y_codes[:].bitcast(FP8X4), scales=y_plane[:, lo:hi], in_=y_bf[:].rearrange("p j t -> p (j t)"))
+            nc.sync.dma_start(words_of(out_1)[:, lo:hi], y_codes[:].bitcast(I32))
         for q in range(4):
             eng = nc.sync if q % 2 else nc.scalar
             eng.dma_start(out_2[0, 4 * q : 4 * q + 4, :].bitcast(I32), y_plane[32 * q : 32 * q + 4, :].bitcast(I32))

@@ -14,13 +14,17 @@ ACT = mybir.ActivationFunctionType
 
 P = 128
 PACK = 4
+QUADS = 4
+GROUP = 16
 S = 512
-HALF = 256
+HALF = S // 2
 TABLE = 2048
 U = 384
-SPARE = 16
-FLOPS = 2 * 2 * 512 * 512 * 512
-CFG = {"E":"SSSS","ga":"VVVV","gb":"SSSS","n":"SSSSSSSS","sc":"SSSSSSSS","zi":"00","il":"VV","F":"SSSSVVVV","P":"YYVS","C":"VV","K":"VVSV","ne":"4","warm":1,"cut":256}
+H_WINDOW = S + GROUP
+Y_WINDOW = 2 * U
+LAST = PACK - 1
+SCALAR_SCATTERS = 2
+FLOPS = 2 * 2 * S * S * S
 
 
 def tile_picked_hpqghopmkgate_none_po_kernel(
@@ -31,8 +35,8 @@ def tile_picked_hpqghopmkgate_none_po_kernel(
         keep = ctx.enter_context(tc.tile_pool(name="keep", bufs=1))
         psum = ctx.enter_context(tc.psum_pool(name="psum", bufs=1))
 
-        def sb(name, shape, dtype):
-            return keep.tile(shape, dtype, name=name, align_bytes=64)
+        def sbuf(name, shape, dtype, tag=""):
+            return keep.tile(shape, dtype, name=name, tag=tag or name, align_bytes=64)
 
         def words_of(dram):
             return dram[0].rearrange("p n t -> p (n t)").bitcast(I32)
@@ -40,203 +44,191 @@ def tile_picked_hpqghopmkgate_none_po_kernel(
         def half(h):
             return slice(HALF * h, HALF * (h + 1))
 
-        k1_t = sb("k1_t", [P, 32], U16)
-        offs_t = sb("offs_t", [P, 32], U16)
-        n1_t = sb("n1_t", [P, 64], U16)
-        n2_t = sb("n2_t", [P, 32], U16)
-        n3_t = sb("n3_t", [P, 24], U16)
-        n4_t = sb("n4_t", [P, 24], U16)
-        d_tab = sb("d_tab", [P, TABLE], U32)
-        x_tab = sb("x_tab", [P, TABLE], U32)
-        d_stab = sb("d_stab", [P, TABLE], U8)
-        x_stab = sb("x_stab", [P, TABLE], U8)
-        w_raw = sb("w_raw", [P, S], U32)
-        w_sraw = sb("w_sraw", [P, S], U8)
-        gain = sb("gain", [P, PACK], F32)
+        def entries(list_tile, first, count):
+            return list_tile[:, first // GROUP : (first + count) // GROUP]
 
-        nc.gpsimd.memset(d_stab[:].bitcast(I32), 0)
-        nc.vector.memset(x_stab[:].bitcast(I32), 0)
-        nc.gpsimd.memset(w_sraw[:].bitcast(I32), 0)
-
-        nc.scalar.dma_start(gain[:], gn.rearrange("(p t) o -> p (t o)", t=PACK))
-        nc.sync.dma_start(k1_t[:], k1)
-        nc.sync.dma_start(offs_t[:], offs)
-        nc.sync.dma_start(d_stab[0:P:8, :].bitcast(I32), d_scales[0].bitcast(I32))
-        nc.sync.dma_start(x_stab[0:P:8, :].bitcast(I32), x_scales[0].bitcast(I32))
-        nc.sync.dma_start(d_tab[:].bitcast(I32), words_of(d_words))
-        nc.sync.dma_start(n1_t[:], n1)
-        nc.sync.dma_start(x_tab[:].bitcast(I32), words_of(x_words))
-
-        warm = sb("warm", [P, 1], F32)
-        nc.scalar.activation(warm[:], gain[:, 0:1], ACT.Sigmoid)
-        d_sg = sb("d_sg", [P, S], U8)
-        x_sg = sb("x_sg", [P, S], U8)
-        planes = sb("planes", [P, 2 * S], U8)
-        nc.vector.tensor_copy(d_sg[:], d_stab[:].indirect(k1_t[:]))
-        nc.vector.tensor_copy(x_sg[:], x_stab[:].indirect(offs_t[:]))
-        nc.vector.tensor_copy(
-            planes[:, 0:S].rearrange("p (t m) -> p t m", t=PACK), d_sg[:].rearrange("p (m t) -> p t m", t=PACK)
-        )
-        nc.vector.tensor_copy(planes[:, S : 2 * S].bitcast(I32), x_sg[:].bitcast(I32))
-        for a in range(1, 4):
-            nc.sync.dma_start(planes[a:P:32, :].bitcast(I32), planes[8 * a : P : 32, :].bitcast(I32))
-
-        nc.sync.dma_start(w_raw[:].bitcast(I32), words_of(w1_words))
-        nc.sync.dma_start(n2_t[:], n2)
-        nc.sync.dma_start(n3_t[:], n3)
-        nc.sync.dma_start(n4_t[:], n4)
-        for q in range(4):
-            nc.sync.dma_start(w_sraw[32 * q : 32 * q + 4, :].bitcast(I32), w1_scales[0, 4 * q : 4 * q + 4, :].bitcast(I32))
-
-        def deal_words(dst, src):
-            nc.vector.tensor_copy(
-                dst[:].rearrange("p (t c i) -> p c t i", t=PACK, i=4), src[:].rearrange("p (c i t) -> p c t i", t=PACK, i=4)
-            )
-
-        d_g = sb("d_g", [P, S], U32)
-        d_dealt = sb("d_dealt", [P, S], U32)
-        x_g = [sb("x_g%d" % h, [P, HALF], U32) for h in range(2)]
-        nc.vector.tensor_copy(d_g[:], d_tab[:].indirect(k1_t[:]))
-        deal_words(d_dealt, d_g)
-        for h in range(2):
-            nc.vector.tensor_copy(x_g[h][:], x_tab[:].indirect(offs_t[:, 16 * h : 16 * (h + 1)]))
-
-        hh = [sb("h%d" % t, [P, S + SPARE], F32) for t in range(PACK)]
-        st = [sb("st%d" % t, [P, S], F32) for t in range(PACK)]
-        for t in range(PACK):
-            nc.vector.memset(hh[t][:, S:], 0.0)
-
-        acc1 = {}
-        for t in range(PACK):
-            for h in range(2):
-                acc1[t, h] = psum.tile([P, HALF], F32, name="acc1_%d_%d" % (t, h), tag="bank%d_%d" % (t, h))
-                nc.tensor.matmul_mx(
-                    out=acc1[t, h][:],
-                    lhsT=d_dealt[:, P * t : P * (t + 1)].bitcast(FP8X4),
-                    lhsT_scale=planes[:, P * t : P * (t + 1)],
-                    rhs=x_g[h][:].bitcast(FP8X4),
-                    rhs_scale=planes[:, S + HALF * h : S + HALF * (h + 1)],
-                    start=True,
-                    stop=True,
-                )
-
-        w_dealt = sb("w_dealt", [P, S], U32)
-        w_plane = sb("w_plane", [P, S], U8)
-        deal_words(w_dealt, w_raw)
-        nc.vector.tensor_copy(
-            w_plane[:].rearrange("p (t m) -> p t m", t=PACK), w_sraw[:].rearrange("p (m t) -> p t m", t=PACK)
-        )
-
-        mb = [sb("mb%d" % t, [P, 2 * S], F32) for t in range(PACK)]
-        mx = [sb("mx%d" % t, [P, S], F32) for t in range(PACK)]
-
-        def gather(eng, out, window, offsets):
-            if eng == "S":
+        def gather(on_scalar, out, window, offsets):
+            if on_scalar:
                 nc.scalar.activation(out, window.indirect(offsets), ACT.Copy)
             else:
                 nc.vector.tensor_copy(out, window.indirect(offsets))
 
-        def scaled(eng, out, in_, scale):
-            if eng == "S":
-                nc.scalar.activation(out, in_, ACT.Copy, scale=scale)
-            else:
-                nc.vector.tensor_scalar(out, in_, scale, None, ALU.mult)
-
-        def copy(eng, out, in_):
-            if eng == "S":
+        def copy(on_scalar, out, in_):
+            if on_scalar:
                 nc.scalar.copy(out, in_)
             else:
                 nc.vector.tensor_copy(out, in_)
 
-        def interleave(eng, out, rows):
-            copy(eng, out.rearrange("p (c i) t -> p c t i", i=4), rows.rearrange("p t (c i) -> p c t i", i=4))
+        def deal_words(dealt, words):
+            nc.vector.tensor_copy(
+                dealt.rearrange("p (t c i) -> p c t i", t=PACK, i=4), words.rearrange("p (c i t) -> p c t i", t=PACK, i=4)
+            )
 
-        def front(t):
+        def deal_bytes(dealt, plane):
+            nc.vector.tensor_copy(dealt.rearrange("p (t m) -> p t m", t=PACK), plane.rearrange("p (m t) -> p t m", t=PACK))
+
+        def interleave(out, rows):
+            nc.vector.tensor_copy(out.rearrange("p (c i) t -> p c t i", i=4), rows.rearrange("p t (c i) -> p c t i", i=4))
+
+        def product(name, t, h, lhs_words, lhs_plane, rhs_words, rhs_plane):
+            acc = psum.tile([P, HALF], F32, name="%s_%d_%d" % (name, t, h), tag="bank%d_%d" % (t, h))
+            nc.tensor.matmul_mx(
+                out=acc[:],
+                lhsT=lhs_words[:, P * t : P * (t + 1)].bitcast(FP8X4),
+                lhsT_scale=lhs_plane[:, P * t : P * (t + 1)],
+                rhs=rhs_words.bitcast(FP8X4),
+                rhs_scale=rhs_plane,
+                start=True,
+                stop=True,
+            )
+            return acc
+
+        k1_list = sbuf("k1_list", [P, S // GROUP], U16)
+        offs_list = sbuf("offs_list", [P, S // GROUP], U16)
+        n1_list = sbuf("n1_list", [P, 2 * S // GROUP], U16)
+        n2_list = sbuf("n2_list", [P, S // GROUP], U16)
+        n3_list = sbuf("n3_list", [P, U // GROUP], U16)
+        n4_list = sbuf("n4_list", [P, U // GROUP], U16)
+        d_table = sbuf("d_table", [P, TABLE], U32)
+        x_table = sbuf("x_table", [P, TABLE], U32, tag="x_table_then_w_scales")
+        d_scale_table = sbuf("d_scale_table", [P, TABLE], U8)
+        x_scale_table = sbuf("x_scale_table", [P, TABLE], U8, tag="x_scale_table_then_planes")
+        w_words = sbuf("w_words", [P, S], U32)
+        gain = sbuf("gain", [P, PACK], F32)
+
+        for scale_table in (d_scale_table, x_scale_table):
+            nc.vector.memset(scale_table[:, 0 : TABLE // 2].bitcast(I32), 0)
+            nc.gpsimd.memset(scale_table[:, TABLE // 2 :].bitcast(I32), 0)
+
+        nc.scalar.dma_start(gain[:], gn.rearrange("(p t) o -> p (t o)", t=PACK))
+        nc.sync.dma_start(k1_list[:], k1)
+        nc.sync.dma_start(offs_list[:], offs)
+        nc.scalar.dma_start(d_scale_table[0:P:8, :].bitcast(I32), d_scales[0].bitcast(I32))
+        nc.sync.dma_start(x_scale_table[0:P:8, :].bitcast(I32), x_scales[0].bitcast(I32))
+        nc.sync.dma_start(d_table[:].bitcast(I32), words_of(d_words))
+        nc.sync.dma_start(n1_list[:], n1)
+        nc.sync.dma_start(x_table[:].bitcast(I32), words_of(x_words))
+
+        warm_up = sbuf("warm_up", [P, 1], F32)
+        nc.scalar.activation(warm_up[:], gain[:, 0:1], ACT.Sigmoid)
+
+        d_scale_picked = sbuf("d_scale_picked", [P, S], U8)
+        x_scale_picked = sbuf("x_scale_picked", [P, S], U8)
+        nc.vector.tensor_copy(d_scale_picked[:], d_scale_table[:].indirect(k1_list[:]))
+        nc.vector.tensor_copy(x_scale_picked[:], x_scale_table[:].indirect(offs_list[:]))
+        planes = sbuf("planes", [P, 2 * S], U8, tag="x_scale_table_then_planes")
+        d_plane, x_plane = planes[:, 0:S], planes[:, S : 2 * S]
+        deal_bytes(d_plane, d_scale_picked[:])
+        nc.vector.tensor_copy(x_plane.bitcast(I32), x_scale_picked[:].bitcast(I32))
+        for a in range(1, 4):
+            nc.scalar.dma_start(planes[a:P:32, :].bitcast(I32), planes[8 * a : P : 32, :].bitcast(I32))
+
+        nc.sync.dma_start(w_words[:].bitcast(I32), words_of(w1_words))
+        nc.sync.dma_start(n2_list[:], n2)
+        nc.sync.dma_start(n3_list[:], n3)
+        nc.sync.dma_start(n4_list[:], n4)
+
+        d_picked = sbuf("d_picked", [P, S], U32)
+        d_dealt = sbuf("d_dealt", [P, S], U32)
+        x_picked = [sbuf("x_picked%d" % h, [P, HALF], U32) for h in range(2)]
+        nc.vector.tensor_copy(d_picked[:], d_table[:].indirect(k1_list[:]))
+        deal_words(d_dealt[:], d_picked[:])
+        for h in range(2):
+            nc.vector.tensor_copy(x_picked[h][:], x_table[:].indirect(entries(offs_list, HALF * h, HALF)))
+
+        w_scales = sbuf("w_scales", [P, S], U8, tag="x_table_then_w_scales")
+        nc.gpsimd.memset(w_scales[:].bitcast(I32), 0)
+        for q in range(QUADS):
+            nc.sync.dma_start(w_scales[32 * q : 32 * q + 4, :].bitcast(I32), w1_scales[0, 4 * q : 4 * q + 4, :].bitcast(I32))
+
+        h_rows = [sbuf("h%d" % t, [P, H_WINDOW], F32) for t in range(PACK)]
+        st = [sbuf("st%d" % t, [P, S], F32) for t in range(PACK)]
+        for t in range(PACK):
+            nc.vector.memset(h_rows[t][:, S:], 0.0)
+
+        h_acc = {}
+        for t in range(PACK):
             for h in range(2):
-                scaled(CFG["E"][t], hh[t][:, half(h)], acc1[t, h][:], 0.0625)
-            gather(CFG["ga"][t], mb[t][:, 0:S], hh[t][:], n1_t[:, 0:32])
-            gather(CFG["gb"][t], mb[t][:, S : 2 * S], hh[t][:], n1_t[:, 32:64])
+                h_acc[t, h] = product("h_acc", t, h, d_dealt, d_plane, x_picked[h][:], x_plane[:, half(h)])
 
-        def mid(t):
+        w_dealt = sbuf("w_dealt", [P, S], U32)
+        w_plane = sbuf("w_plane", [P, S], U8)
+        deal_words(w_dealt[:], w_words[:])
+        deal_bytes(w_plane[:], w_scales[:])
+
+        mb = [sbuf("mb%d" % t, [P, 2 * S], F32) for t in range(PACK)]
+        mx = [sbuf("mx%d" % t, [P, S], F32) for t in range(PACK)]
+
+        def fetch_members(t):
+            for h in range(2):
+                if t == LAST:
+                    nc.vector.tensor_scalar(h_rows[t][:, half(h)], h_acc[t, h][:], 0.0625, None, ALU.mult)
+                else:
+                    nc.scalar.activation(h_rows[t][:, half(h)], h_acc[t, h][:], ACT.Copy, scale=0.0625)
+            gather(t == LAST, mb[t][:, 0:S], h_rows[t][:], entries(n1_list, 0, S))
+            gather(True, mb[t][:, S : 2 * S], h_rows[t][:], entries(n1_list, S, S))
+
+        def subtract_larger_member(t):
             pairs = mb[t][:].rearrange("p (j two) -> p j two", two=2)
             nc.vector.tensor_tensor(mx[t][:], pairs[:, :, 0], pairs[:, :, 1], ALU.max)
-            nc.vector.tensor_tensor(st[t][:], hh[t][:, 0:S], mx[t][:], ALU.subtract)
+            nc.vector.tensor_tensor(st[t][:], h_rows[t][:, 0:S], mx[t][:], ALU.subtract)
 
-        for s in range(PACK + 1):
-            if s < PACK:
-                front(s)
-            if s > 0:
-                mid(s - 1)
+        for step in range(PACK + 1):
+            if step < PACK:
+                fetch_members(step)
+            if step > 0:
+                subtract_larger_member(step - 1)
 
-        y = [sb("y%d" % t, [P, 2 * U], F32) for t in range(PACK)]
+        y = [sbuf("y%d" % t, [P, Y_WINDOW], F32) for t in range(PACK)]
         for t in range(PACK):
             nc.vector.memset(y[t][:, S:], 0.0)
-        for h in range(2):
-            z_rows = sb("z_rows%d" % h, [P, PACK, HALF], BF16)
-            z = sb("z%d" % h, [P, HALF, PACK], BF16)
-            z_codes = sb("z_codes%d" % h, [P, HALF], U32)
-            z_plane = sb("z_plane%d" % h, [P, HALF], U8)
-            big = sb("big%d" % h, [P, PACK, HALF], F32)
-            for t in range(PACK):
-                other = sb("other%d_%d" % (t, h), [P, HALF], F32)
-                gather(CFG["n"][4 * h + t], other[:], st[t][:], n2_t[:, 16 * h : 16 * (h + 1)])
-                nc.vector.tensor_tensor(big[:, t, :], st[t][:, half(h)], other[:], ALU.max)
-                if CFG["zi"][h] == "0":
-                    scaled(CFG["sc"][4 * h + t], z_rows[:, t, :], big[:, t, :], gain[:, t : t + 1])
-            if CFG["zi"][h] == "0":
-                interleave(CFG["il"][h], z[:], z_rows[:])
-            else:
-                nc.vector.tensor_tensor(
-                    z[:].rearrange("p (c i) t -> p c t i", i=4),
-                    big[:].rearrange("p t (c i) -> p c t i", i=4),
-                    gain[:].unsqueeze(1).unsqueeze(3).to_broadcast([P, HALF // 4, PACK, 4]),
-                    ALU.mult,
-                )
-            nc.vector.quantize_mx(out=z_codes[:].bitcast(FP8X4), scales=z_plane[:], in_=z[:].rearrange("p j t -> p (j t)"))
-            acc2 = []
-            for t in range(PACK):
-                acc = psum.tile([P, HALF], F32, name="acc2_%d_%d" % (t, h), tag="bank%d_%d" % (t, h))
-                acc2.append(acc)
-                nc.tensor.matmul_mx(
-                    out=acc[:],
-                    lhsT=w_dealt[:, P * t : P * (t + 1)].bitcast(FP8X4),
-                    lhsT_scale=w_plane[:, P * t : P * (t + 1)],
-                    rhs=z_codes[:].bitcast(FP8X4),
-                    rhs_scale=z_plane[:],
-                    start=True,
-                    stop=True,
-                )
-            for t in range(PACK):
-                copy(CFG["F"][4 * h + t], y[t][:, half(h)], acc2[t][:])
 
-        old = [sb("old%d" % t, [P, U], F32) for t in range(PACK)]
-        gate = [sb("gate%d" % t, [P, U], F32) for t in range(PACK)]
-        y_rows = sb("y_rows", [P, PACK, S], BF16)
+        for h in range(2):
+            z_rows = sbuf("z_rows%d" % h, [P, PACK, HALF], BF16)
+            z = sbuf("z%d" % h, [P, HALF, PACK], BF16)
+            z_words = sbuf("z_words%d" % h, [P, HALF], U32)
+            z_plane = sbuf("z_plane%d" % h, [P, HALF], U8)
+            larger = sbuf("larger%d" % h, [P, PACK, HALF], F32)
+            for t in range(PACK):
+                partner = sbuf("partner%d_%d" % (t, h), [P, HALF], F32)
+                gather(t > 0 or h > 0, partner[:], st[t][:], entries(n2_list, HALF * h, HALF))
+                nc.vector.tensor_tensor(larger[:, t, :], st[t][:, half(h)], partner[:], ALU.max)
+                nc.scalar.activation(z_rows[:, t, :], larger[:, t, :], ACT.Copy, scale=gain[:, t : t + 1])
+            interleave(z[:], z_rows[:])
+            nc.vector.quantize_mx(out=z_words[:].bitcast(FP8X4), scales=z_plane[:], in_=z[:].rearrange("p j t -> p (j t)"))
+            h2_acc = [product("h2_acc", t, h, w_dealt, w_plane, z_words[:], z_plane[:]) for t in range(PACK)]
+            for t in range(PACK):
+                copy(h == 0, y[t][:, half(h)], h2_acc[t][:])
+
+        fetched = [sbuf(("ra%d" if t < SCALAR_SCATTERS else "old%d") % t, [P, U], F32) for t in range(PACK)]
+        gate = [sbuf("gate%d" % t, [P, U], F32) for t in range(PACK)]
+        y_rows = sbuf("y_rows", [P, PACK, S], BF16)
         out_rows = out_0.rearrange("(p t) j -> p t j", t=PACK)
         for t in range(PACK):
-            nc.scalar.activation(gate[t][:], y[t][:].indirect(n4_t[:]), ACT.Sigmoid)
-            if CFG["P"][t] == "Y":
-                nc.vector.tensor_tensor(old[t][:], y[t][:].indirect(n3_t[:]), gate[t][:], ALU.mult)
+            nc.scalar.activation(gate[t][:], y[t][:].indirect(n4_list[:]), ACT.Sigmoid)
+            if t < SCALAR_SCATTERS:
+                nc.vector.tensor_tensor(fetched[t][:], y[t][:].indirect(n3_list[:]), gate[t][:], ALU.mult)
             else:
-                gather(CFG["P"][t], old[t][:], y[t][:], n3_t[:])
+                gather(t == LAST, fetched[t][:], y[t][:], n3_list[:])
         for t in range(PACK):
-            if CFG["P"][t] == "Y":
-                nc.scalar.activation(y[t][:].indirect(n3_t[:]), old[t][:], ACT.Copy)
+            if t < SCALAR_SCATTERS:
+                nc.scalar.activation(y[t][:].indirect(n3_list[:]), fetched[t][:], ACT.Copy)
             else:
-                nc.vector.tensor_tensor(y[t][:].indirect(n3_t[:]), old[t][:], gate[t][:], ALU.mult)
+                nc.vector.tensor_tensor(y[t][:].indirect(n3_list[:]), fetched[t][:], gate[t][:], ALU.mult)
             nc.sync.dma_start(out_rows[:, t, :], y[t][:, 0:S])
-        early = int(CFG["ne"])
-        for t in range(early):
-            copy(CFG["K"][t], y_rows[:, t, :], y[t][:, 0:S])
 
-        y_plane = sb("y_plane", [P, S], U8)
-        cut = CFG["cut"]
-        for h, (lo, hi) in enumerate([(0, cut), (cut, S)]):
-            y_bf = sb("y_bf%d" % h, [P, hi - lo, PACK], BF16)
-            y_codes = sb("y_codes%d" % h, [P, hi - lo], U32)
-            interleave(CFG["C"][h], y_bf[:], y_rows[:, :, lo:hi])
-            nc.vector.quantize_mx(out=y_codes[:].bitcast(FP8X4), scales=y_plane[:, lo:hi], in_=y_bf[:].rearrange("p j t -> p (j t)"))
-            nc.sync.dma_start(words_of(out_1)[:, lo:hi], y_codes[:].bitcast(I32))
-        for q in range(4):
-            eng = nc.sync if q % 2 else nc.scalar
-            eng.dma_start(out_2[0, 4 * q : 4 * q + 4, :].bitcast(I32), y_plane[32 * q : 32 * q + 4, :].bitcast(I32))
+        for t in range(PACK):
+            copy(t == SCALAR_SCATTERS, y_rows[:, t, :], y[t][:, 0:S])
+
+        y_plane = sbuf("y_plane", [P, S], U8)
+        for h in range(2):
+            y_interleaved = sbuf("y_interleaved%d" % h, [P, HALF, PACK], BF16)
+            y_words = sbuf("y_words%d" % h, [P, HALF], U32)
+            interleave(y_interleaved[:], y_rows[:, :, half(h)])
+            nc.vector.quantize_mx(
+                out=y_words[:].bitcast(FP8X4), scales=y_plane[:, half(h)], in_=y_interleaved[:].rearrange("p j t -> p (j t)")
+            )
+            nc.sync.dma_start(words_of(out_1)[:, half(h)], y_words[:].bitcast(I32))
+        for q in range(QUADS):
+            queue = nc.sync if q % 2 else nc.scalar
+            queue.dma_start(out_2[0, 4 * q : 4 * q + 4, :].bitcast(I32), y_plane[32 * q : 32 * q + 4, :].bitcast(I32))

from contextlib import ExitStack

import concourse.mybir as mybir

F32 = mybir.dt.float32
BF16 = mybir.dt.bfloat16
U32 = mybir.dt.uint32
I32 = mybir.dt.int32
U16 = mybir.dt.uint16
U8 = mybir.dt.uint8
FP8X4 = mybir.dt.float8_e4m3fn_x4
ALU = mybir.AluOpType
ACT = mybir.ActivationFunctionType

P = 128
PACK = 4
QUADS = 4
GROUP = 16
S = 512
HALF = S // 2
TABLE = 2048
U = 384
H_WINDOW = S + GROUP
Y_WINDOW = 2 * U
LAST = PACK - 1
SCALAR_SCATTERS = 2
FLOPS = 2 * 2 * S * S * S


def tile_picked_hpqghopmkgate_none_po_kernel(
    tc, x_words, x_scales, d_words, d_scales, gn, w1_words, w1_scales, offs, k1, n1, n2, n3, n4, out_0, out_1, out_2
):
    nc = tc.nc
    with ExitStack() as ctx:
        keep = ctx.enter_context(tc.tile_pool(name="keep", bufs=1))
        psum = ctx.enter_context(tc.psum_pool(name="psum", bufs=1))

        def sbuf(name, shape, dtype, tag=""):
            return keep.tile(shape, dtype, name=name, tag=tag or name, align_bytes=64)

        def words_of(dram):
            return dram[0].rearrange("p n t -> p (n t)").bitcast(I32)

        def half(h):
            return slice(HALF * h, HALF * (h + 1))

        def entries(list_tile, first, count):
            return list_tile[:, first // GROUP : (first + count) // GROUP]

        def gather(on_scalar, out, window, offsets):
            if on_scalar:
                nc.scalar.activation(out, window.indirect(offsets), ACT.Copy)
            else:
                nc.vector.tensor_copy(out, window.indirect(offsets))

        def copy(on_scalar, out, in_):
            if on_scalar:
                nc.scalar.copy(out, in_)
            else:
                nc.vector.tensor_copy(out, in_)

        def deal_words(dealt, words):
            nc.vector.tensor_copy(
                dealt.rearrange("p (t c i) -> p c t i", t=PACK, i=4), words.rearrange("p (c i t) -> p c t i", t=PACK, i=4)
            )

        def deal_bytes(dealt, plane):
            nc.vector.tensor_copy(dealt.rearrange("p (t m) -> p t m", t=PACK), plane.rearrange("p (m t) -> p t m", t=PACK))

        def interleave(out, rows):
            nc.vector.tensor_copy(out.rearrange("p (c i) t -> p c t i", i=4), rows.rearrange("p t (c i) -> p c t i", i=4))

        def product(name, t, h, lhs_words, lhs_plane, rhs_words, rhs_plane):
            acc = psum.tile([P, HALF], F32, name="%s_%d_%d" % (name, t, h), tag="bank%d_%d" % (t, h))
            nc.tensor.matmul_mx(
                out=acc[:],
                lhsT=lhs_words[:, P * t : P * (t + 1)].bitcast(FP8X4),
                lhsT_scale=lhs_plane[:, P * t : P * (t + 1)],
                rhs=rhs_words.bitcast(FP8X4),
                rhs_scale=rhs_plane,
                start=True,
                stop=True,
            )
            return acc

        k1_list = sbuf("k1_list", [P, S // GROUP], U16)
        offs_list = sbuf("offs_list", [P, S // GROUP], U16)
        n1_list = sbuf("n1_list", [P, 2 * S // GROUP], U16)
        n2_list = sbuf("n2_list", [P, S // GROUP], U16)
        n3_list = sbuf("n3_list", [P, U // GROUP], U16)
        n4_list = sbuf("n4_list", [P, U // GROUP], U16)
        d_table = sbuf("d_table", [P, TABLE], U32)
        x_table = sbuf("x_table", [P, TABLE], U32, tag="x_table_then_w_scales")
        d_scale_table = sbuf("d_scale_table", [P, TABLE], U8)
        x_scale_table = sbuf("x_scale_table", [P, TABLE], U8, tag="x_scale_table_then_planes")
        w_words = sbuf("w_words", [P, S], U32)
        gain = sbuf("gain", [P, PACK], F32)

        for scale_table in (d_scale_table, x_scale_table):
            nc.vector.memset(scale_table[:, 0 : TABLE // 2].bitcast(I32), 0)
            nc.gpsimd.memset(scale_table[:, TABLE // 2 :].bitcast(I32), 0)

        nc.scalar.dma_start(gain[:], gn.rearrange("(p t) o -> p (t o)", t=PACK))
        nc.sync.dma_start(k1_list[:], k1)
        nc.sync.dma_start(offs_list[:], offs)
        nc.scalar.dma_start(d_scale_table[0:P:8, :].bitcast(I32), d_scales[0].bitcast(I32))
        nc.sync.dma_start(x_scale_table[0:P:8, :].bitcast(I32), x_scales[0].bitcast(I32))
        nc.sync.dma_start(d_table[:].bitcast(I32), words_of(d_words))
        nc.sync.dma_start(n1_list[:], n1)
        nc.sync.dma_start(x_table[:].bitcast(I32), words_of(x_words))

        warm_up = sbuf("warm_up", [P, 1], F32)
        nc.scalar.activation(warm_up[:], gain[:, 0:1], ACT.Sigmoid)

        d_scale_picked = sbuf("d_scale_picked", [P, S], U8)
        x_scale_picked = sbuf("x_scale_picked", [P, S], U8)
        nc.vector.tensor_copy(d_scale_picked[:], d_scale_table[:].indirect(k1_list[:]))
        nc.vector.tensor_copy(x_scale_picked[:], x_scale_table[:].indirect(offs_list[:]))
        planes = sbuf("planes", [P, 2 * S], U8, tag="x_scale_table_then_planes")
        d_plane, x_plane = planes[:, 0:S], planes[:, S : 2 * S]
        deal_bytes(d_plane, d_scale_picked[:])
        nc.vector.tensor_copy(x_plane.bitcast(I32), x_scale_picked[:].bitcast(I32))
        for a in range(1, 4):
            nc.scalar.dma_start(planes[a:P:32, :].bitcast(I32), planes[8 * a : P : 32, :].bitcast(I32))

        nc.sync.dma_start(w_words[:].bitcast(I32), words_of(w1_words))
        nc.sync.dma_start(n2_list[:], n2)
        nc.sync.dma_start(n3_list[:], n3)
        nc.sync.dma_start(n4_list[:], n4)

        d_picked = sbuf("d_picked", [P, S], U32)
        d_dealt = sbuf("d_dealt", [P, S], U32)
        x_picked = [sbuf("x_picked%d" % h, [P, HALF], U32) for h in range(2)]
        nc.vector.tensor_copy(d_picked[:], d_table[:].indirect(k1_list[:]))
        deal_words(d_dealt[:], d_picked[:])
        for h in range(2):
            nc.vector.tensor_copy(x_picked[h][:], x_table[:].indirect(entries(offs_list, HALF * h, HALF)))

        w_scales = sbuf("w_scales", [P, S], U8, tag="x_table_then_w_scales")
        nc.gpsimd.memset(w_scales[:].bitcast(I32), 0)
        for q in range(QUADS):
            nc.sync.dma_start(w_scales[32 * q : 32 * q + 4, :].bitcast(I32), w1_scales[0, 4 * q : 4 * q + 4, :].bitcast(I32))

        h_rows = [sbuf("h%d" % t, [P, H_WINDOW], F32) for t in range(PACK)]
        st = [sbuf("st%d" % t, [P, S], F32) for t in range(PACK)]
        for t in range(PACK):
            nc.vector.memset(h_rows[t][:, S:], 0.0)

        h_acc = {}
        for t in range(PACK):
            for h in range(2):
                h_acc[t, h] = product("h_acc", t, h, d_dealt, d_plane, x_picked[h][:], x_plane[:, half(h)])

        w_dealt = sbuf("w_dealt", [P, S], U32)
        w_plane = sbuf("w_plane", [P, S], U8)
        deal_words(w_dealt[:], w_words[:])
        deal_bytes(w_plane[:], w_scales[:])

        mb = [sbuf("mb%d" % t, [P, 2 * S], F32) for t in range(PACK)]
        mx = [sbuf("mx%d" % t, [P, S], F32) for t in range(PACK)]

        def fetch_members(t):
            for h in range(2):
                if t == LAST:
                    nc.vector.tensor_scalar(h_rows[t][:, half(h)], h_acc[t, h][:], 0.0625, None, ALU.mult)
                else:
                    nc.scalar.activation(h_rows[t][:, half(h)], h_acc[t, h][:], ACT.Copy, scale=0.0625)
            gather(t == LAST, mb[t][:, 0:S], h_rows[t][:], entries(n1_list, 0, S))
            gather(True, mb[t][:, S : 2 * S], h_rows[t][:], entries(n1_list, S, S))

        def subtract_larger_member(t):
            pairs = mb[t][:].rearrange("p (j two) -> p j two", two=2)
            nc.vector.tensor_tensor(mx[t][:], pairs[:, :, 0], pairs[:, :, 1], ALU.max)
            nc.vector.tensor_tensor(st[t][:], h_rows[t][:, 0:S], mx[t][:], ALU.subtract)

        for step in range(PACK + 1):
            if step < PACK:
                fetch_members(step)
            if step > 0:
                subtract_larger_member(step - 1)

        y = [sbuf("y%d" % t, [P, Y_WINDOW], F32) for t in range(PACK)]
        for t in range(PACK):
            nc.vector.memset(y[t][:, S:], 0.0)

        for h in range(2):
            z_rows = sbuf("z_rows%d" % h, [P, PACK, HALF], BF16)
            z = sbuf("z%d" % h, [P, HALF, PACK], BF16)
            z_words = sbuf("z_words%d" % h, [P, HALF], U32)
            z_plane = sbuf("z_plane%d" % h, [P, HALF], U8)
            larger = sbuf("larger%d" % h, [P, PACK, HALF], F32)
            for t in range(PACK):
                partner = sbuf("partner%d_%d" % (t, h), [P, HALF], F32)
                gather(t > 0 or h > 0, partner[:], st[t][:], entries(n2_list, HALF * h, HALF))
                nc.vector.tensor_tensor(larger[:, t, :], st[t][:, half(h)], partner[:], ALU.max)
                nc.scalar.activation(z_rows[:, t, :], larger[:, t, :], ACT.Copy, scale=gain[:, t : t + 1])
            interleave(z[:], z_rows[:])
            nc.vector.quantize_mx(out=z_words[:].bitcast(FP8X4), scales=z_plane[:], in_=z[:].rearrange("p j t -> p (j t)"))
            h2_acc = [product("h2_acc", t, h, w_dealt, w_plane, z_words[:], z_plane[:]) for t in range(PACK)]
            for t in range(PACK):
                copy(h == 0, y[t][:, half(h)], h2_acc[t][:])

        fetched = [sbuf(("ra%d" if t < SCALAR_SCATTERS else "old%d") % t, [P, U], F32) for t in range(PACK)]
        gate = [sbuf("gate%d" % t, [P, U], F32) for t in range(PACK)]
        y_rows = sbuf("y_rows", [P, PACK, S], BF16)
        out_rows = out_0.rearrange("(p t) j -> p t j", t=PACK)
        for t in range(PACK):
            nc.scalar.activation(gate[t][:], y[t][:].indirect(n4_list[:]), ACT.Sigmoid)
            if t < SCALAR_SCATTERS:
                nc.vector.tensor_tensor(fetched[t][:], y[t][:].indirect(n3_list[:]), gate[t][:], ALU.mult)
            else:
                gather(t == LAST, fetched[t][:], y[t][:], n3_list[:])
        for t in range(PACK):
            if t < SCALAR_SCATTERS:
                nc.scalar.activation(y[t][:].indirect(n3_list[:]), fetched[t][:], ACT.Copy)
            else:
                nc.vector.tensor_tensor(y[t][:].indirect(n3_list[:]), fetched[t][:], gate[t][:], ALU.mult)
            nc.sync.dma_start(out_rows[:, t, :], y[t][:, 0:S])

        for t in range(PACK):
            copy(t == SCALAR_SCATTERS, y_rows[:, t, :], y[t][:, 0:S])

        y_plane = sbuf("y_plane", [P, S], U8)
        for h in range(2):
            y_interleaved = sbuf("y_interleaved%d" % h, [P, HALF, PACK], BF16)
            y_words = sbuf("y_words%d" % h, [P, HALF], U32)
            interleave(y_interleaved[:], y_rows[:, :, half(h)])
            nc.vector.quantize_mx(
                out=y_words[:].bitcast(FP8X4), scales=y_plane[:, half(h)], in_=y_interleaved[:].rearrange("p j t -> p (j t)")
            )
            nc.sync.dma_start(words_of(out_1)[:, half(h)], y_words[:].bitcast(I32))
        for q in range(QUADS):
            queue = nc.sync if q % 2 else nc.scalar
            queue.dma_start(out_2[0, 4 * q : 4 * q + 4, :].bitcast(I32), y_plane[32 * q : 32 * q + 4, :].bitcast(I32))
